import numpy as np
import ml_dtypes


def mxq(x, axis, fmt="e4m3"):
    dtype, down = {"e4m3": (ml_dtypes.float8_e4m3fn, 7), "e5m2": (ml_dtypes.float8_e5m2, 14)}[fmt]
    v = np.moveaxis(np.asarray(x, np.float32).astype(ml_dtypes.bfloat16).astype(np.float64), axis, -1)
    blocks = v.reshape(v.shape[:-1] + (-1, 32))
    amax = np.abs(blocks).max(-1, keepdims=True)
    byte = np.maximum(np.where(amax > 0, np.frexp(amax)[1] - 1 + 127, 0) - down, 1)
    scale = np.exp2(byte - 127.0)
    codes = (blocks / scale).astype(np.float32).astype(dtype).astype(np.float64)
    return np.moveaxis((codes * scale).reshape(v.shape), -1, axis)


WIDE = False


def mx_kscale(k):
    if not WIDE:
        return np.ones(k)
    levels = np.array([10, -10, 5, -5, 0])
    if k % 512:
        return np.exp2(np.random.permutation(np.resize(levels, k // 32))).repeat(32)
    a = np.empty((k // 512, 16))
    for p in range(k // 512):
        a[p, :8] = np.random.permutation(np.resize(levels, 8))
        for g in range(8):
            far = levels[np.abs(levels - a[p, g]) >= 10]
            a[p, g + 8] = far[np.random.randint(len(far))]
    return np.exp2(a.ravel()).repeat(32)


def f64(x):
    return np.asarray(x).astype(np.float64)


def striped(idx):
    return np.tile(np.asarray(idx).reshape(-1, 16).T, (8, 1)).astype(np.uint16)


def unstriped(offs):
    return offs[:16].T.reshape(-1).astype(np.int64)


E2M1 = np.array([0.0, 0.5, 1.0, 1.5, 2.0, 3.0, 4.0, 6.0, -0.0, -0.5, -1.0, -1.5, -2.0, -3.0, -4.0, -6.0])


def pack_weight(w, fmt):
    k, n = w.shape
    w = f64(np.asarray(w, np.float32).astype(ml_dtypes.bfloat16)).reshape(k // 32, 32, n)
    amax = np.abs(w).max(1)
    if fmt == "e4m3":
        byte = np.frexp(amax)[1] - 1 + 127 - 7
    else:
        mant, ex = np.frexp(amax / 6.0)
        byte = np.where(mant > 0.5, ex, ex - 1) + 127
    byte = np.clip(np.where(amax > 0, byte, 1), 1, 254)
    scaled = (w * np.exp2(127.0 - byte)[:, None, :]).reshape(k, n).astype(np.float32)
    by_word = np.ascontiguousarray(scaled.reshape(k // 512, 128, 4, n).transpose(0, 1, 3, 2))
    if fmt == "e4m3":
        words = by_word.astype(ml_dtypes.float8_e4m3fn).view(np.uint8)
    else:
        c = by_word.astype(ml_dtypes.float4_e2m1fn).view(np.uint8) & 0xF
        words = (c[..., 0::2] | (c[..., 1::2] << 4)).reshape(k // 512, 128, 2 * n)
    return np.ascontiguousarray(words), np.ascontiguousarray(byte.astype(np.uint8).reshape(k // 512, 16, n))


def unpack_weight(words, scales, fmt):
    g, _, n = scales.shape
    words = np.ascontiguousarray(words).reshape(g, 128, n, -1)
    if fmt == "e4m3":
        vals = words.view(ml_dtypes.float8_e4m3fn).astype(np.float64)
    else:
        nib = np.empty((g, 128, n, 4), np.uint8)
        nib[..., 0::2] = words & 0xF
        nib[..., 1::2] = words >> 4
        vals = E2M1[nib]
    vals = vals * np.repeat(np.exp2(scales.astype(np.float64) - 127.0), 8, axis=1)[..., None]
    return vals.transpose(0, 1, 3, 2).reshape(g * 512, n)


def bf(x):
    return np.asarray(x, np.float32).astype(ml_dtypes.bfloat16)


def planes(Y):
    r, m = Y.shape
    b = f64(bf(Y)).reshape(r // 32, 32, m)
    amax = np.abs(b).max(1)
    byte = np.clip(np.where(amax > 0, np.frexp(amax)[1] - 1 + 127 - 7, 1), 1, 254)
    codes = (b * np.exp2(127.0 - byte)[:, None, :]).reshape(r, m).astype(np.float32).astype(ml_dtypes.float8_e4m3fn).view(np.uint8)
    words = codes.reshape(r // 512, 128, 4, m).transpose(0, 1, 3, 2)
    return np.ascontiguousarray(words), np.ascontiguousarray(byte.astype(np.uint8).reshape(r // 512, 16, m))


D, E, T, I, Q, G = 512, 512, 2048, 512, 512, 64


def setup_inputs():
    n = np.random.standard_normal
    idx = np.random.permutation(T)[:I]
    fd = mx_kscale(D)
    fe = mx_kscale(E)
    keysp = pack_weight(n((D, T)) / fd[:, None], "e2m1")
    valsp = pack_weight(n((E, T)) / fe[:, None], "e2m1")
    return {
        "query": (n((D, Q)) * 0.7 / np.sqrt(D) * fd[:, None]).astype(np.float32),
        "keys_words": keysp[0],
        "keys_scales": keysp[1],
        "lse": (np.random.uniform(6.2, 6.5, (1, Q))).astype(np.float32),
        "mult": (np.random.uniform(20.0, 120.0, (1, Q))).astype(np.float32),
        "gout": (n((E, Q)) * 1 / np.sqrt(E) * fe[:, None]).astype(np.float32),
        "vals_words": valsp[0],
        "vals_scales": valsp[1],
        "old": (np.random.uniform(0.0, 8.0, (I, G))).astype(np.float32),
        "fade": (np.random.uniform(0.5, 1.0, (I, 1))).astype(np.float32),
        "offs": striped(idx),
    }


def reference(query, keys_words, keys_scales, lse, mult, gout, vals_words, vals_scales, old, fade, offs):
    idx = unstriped(offs)
    keysu = unpack_weight(keys_words, keys_scales, "e2m1")
    valsu = unpack_weight(vals_words, vals_scales, "e2m1")
    keysidxg = keysu[:, idx]
    queryq = mxq(f64(query), 0, "e4m3")
    a = keysidxg.T @ queryq
    valsidxg = valsu[:, idx]
    goutq = mxq(f64(gout), 0, "e4m3")
    dp = valsidxg.T @ goutq
    p = np.exp(a - f64(lse))
    cv = p * (1.0 - p * f64(mult)) * np.square(dp) * 512.0
    y = cv.reshape(I, G, Q // G).sum(axis=2) + f64(old) * f64(fade)
    words, scales = planes(y)
    return y, words, scales

@@ -1,0 +1,185 @@
+from contextlib import ExitStack
+
+import concourse.mybir as mybir
+from concourse.masks import make_identity
+
+F32 = mybir.dt.float32
+BF16 = mybir.dt.bfloat16
+I32 = mybir.dt.int32
+U32 = mybir.dt.uint32
+U16 = mybir.dt.uint16
+U8 = mybir.dt.uint8
+FP8X4 = mybir.dt.float8_e4m3fn_x4
+FP4X4 = mybir.dt.float4_e2m1fn_x4
+ACT = mybir.ActivationFunctionType
+ALU = mybir.AluOpType
+
+P = 128
+PACK = 4
+TOKENS = 2048
+SLOTS = 512
+ROWS = 512
+GROUPS = 64
+TILES = ROWS // P
+HALF = ROWS // 2
+SHARE = 96
+FLOPS = 2 * 2 * 512 * SLOTS * ROWS
+
+
+def tile_attend_curvatures_pl_kernel(tc, query, keys_words, keys_scales, lse, mult, gout, vals_words, vals_scales,
+                                      old, fade, offs, out_0, out_1, out_2):
+    nc = tc.nc
+    with ExitStack() as ctx:
+        keep = ctx.enter_context(tc.tile_pool(name="keep", bufs=1))
+        shared = ctx.enter_context(tc.tile_pool(name="shared", bufs=1))
+        psum = ctx.enter_context(tc.psum_pool(name="psum", bufs=1))
+
+        offsets = keep.tile([P, SLOTS // 16], U16, name="offsets")
+        nc.sync.dma_start(offsets[:], offs)
+
+        def load_words(words, name, tag):
+            pool_words = keep.tile([P, TOKENS], U16, name=name, tag=tag, align_bytes=64)
+            nc.sync.dma_start(out=pool_words[:].bitcast(I32), in_=words[0].bitcast(I32))
+            return pool_words
+
+        def load_scales(scales, name, zero_engine, queue):
+            pool_scales = keep.tile([P, TOKENS], U8, name=name, tag=name, align_bytes=64)
+            zero_engine.memset(pool_scales[:].bitcast(I32), 0)
+            for quad in range(4):
+                queue.dma_start(out=pool_scales[32 * quad: 32 * quad + 4, :].bitcast(I32),
+                                in_=scales[0, 4 * quad: 4 * quad + 4, :].bitcast(I32))
+            return pool_scales
+
+        def load_half(src, half, name, tag):
+            raw = keep.tile([P, PACK, HALF], F32, name=name, tag=tag, align_bytes=64)
+            nc.sync.dma_start(out=raw[:], in_=src[:, half * HALF: (half + 1) * HALF].rearrange("(p t) q -> p t q", t=PACK))
+            return raw
+
+        def gather(window, picked):
+            nc.vector.tensor_copy(picked[:], window[:].indirect(offsets[:]))
+            return picked
+
+        def deal_views(grouped, raw, half, c0=0, c1=HALF):
+            m0, m1 = (half * HALF + c0) // TILES, (half * HALF + c1) // TILES
+            dst = grouped[:, :, m0:m1, :].rearrange("p j m t -> p m j t")
+            src = raw[:, :, c0:c1].rearrange("p t (m j) -> p m j t", j=TILES)
+            return dst, src
+
+        def quantise(grouped, codes, scales, j0, j1):
+            nc.vector.quantize_mx(out=codes[:, j0 * P: j1 * P].bitcast(FP8X4), scales=scales[:, j0 * P: j1 * P],
+                                  in_=grouped[:, j0:j1, :, :].rearrange("p j m t -> p (j m t)"))
+
+        def product(codes, scales, words, word_scales, j, tag):
+            bank = psum.tile([P, SLOTS], F32, name="bank_%s" % tag, tag=tag)
+            nc.tensor.matmul_mx(out=bank[:], lhsT=codes[:, j * P: (j + 1) * P].bitcast(FP8X4),
+                                lhsT_scale=scales[:, j * P: (j + 1) * P], rhs=words[:].bitcast(FP4X4),
+                                rhs_scale=word_scales[:], start=True, stop=True)
+            return bank[:].rearrange("p (s t) -> p t s", t=PACK)
+
+        warm = keep.tile([P, 2], F32, name="warm")
+        nc.gpsimd.memset(warm[:, 0:1], 0.0)
+        nc.scalar.activation(warm[:, 1:2], warm[:, 0:1], ACT.Exp)
+        lse_col = keep.tile([P, TILES], F32, name="lse_col", tag="stage1", align_bytes=64)
+        mult_col = keep.tile([P, TILES], F32, name="mult_col", tag="stage2", align_bytes=64)
+        nc.scalar.dma_start(out=lse_col[:], in_=lse.rearrange("o (p j) -> p (o j)", j=TILES))
+        nc.scalar.dma_start(out=mult_col[:], in_=mult.rearrange("o (p j) -> p (o j)", j=TILES))
+
+        k_pool = load_words(keys_words, "k_pool", "stage3")
+        ks_pool = load_scales(keys_scales, "ks_pool", nc.gpsimd, nc.scalar)
+        q_raw = [load_half(query, 0, "q_raw0", "stage0")]
+        vs_pool = load_scales(vals_scales, "vs_pool", nc.vector, nc.scalar)
+
+        neg_lse = keep.tile([P, TILES], F32, name="neg_lse")
+        neg_mult = keep.tile([P, TILES], F32, name="neg_mult")
+        nc.vector.tensor_scalar(neg_lse[:], lse_col[:], -1.0, None, ALU.mult)
+        nc.vector.tensor_scalar(neg_mult[:], mult_col[:], -512.0, None, ALU.mult)
+        q_raw.append(load_half(query, 1, "q_raw1", "stage1"))
+        g_raw = [load_half(gout, 0, "g_raw0", "stage2")]
+
+        k_words = gather(k_pool, keep.tile([P, SLOTS], U16, name="k_words", align_bytes=64))
+        k_scales = gather(ks_pool, keep.tile([P, SLOTS], U8, name="k_scales", align_bytes=64))
+        g_raw.append(load_half(gout, 1, "g_raw1", "stage3"))
+
+        q_grouped = shared.tile([P, TILES, P, PACK], BF16, name="q_grouped", align_bytes=64, offset=0)
+        dst, src = deal_views(q_grouped, q_raw[0], 0)
+        nc.scalar.activation(dst, src, ACT.Copy)
+        v_pool = load_words(vals_words, "v_pool", "stage0")
+        dst, src = deal_views(q_grouped, q_raw[1], 1, 0, SHARE)
+        nc.scalar.activation(dst, src, ACT.Copy)
+        dst, src = deal_views(q_grouped, q_raw[1], 1, SHARE, HALF)
+        nc.vector.tensor_copy(dst, src)
+        old_rows = keep.tile([P, PACK, GROUPS], F32, name="old_rows", tag="stage1", align_bytes=64)
+        nc.sync.dma_start(out=old_rows[:], in_=old.rearrange("(p t) g -> p t g", t=PACK))
+
+        identity = keep.tile([P, P], F32, name="identity")
+        make_identity(nc, identity[:])
+
+        q_codes = keep.tile([P, ROWS], U32, name="q_codes", align_bytes=64)
+        q_scales = keep.tile([P, ROWS], U8, name="q_scales", align_bytes=64)
+        quantise(q_grouped, q_codes, q_scales, 0, 2)
+        quantise(q_grouped, q_codes, q_scales, 2, 4)
+        v_scales = gather(vs_pool, shared.tile([P, SLOTS], U8, name="v_scales", align_bytes=64, offset=0))
+
+        g_grouped = shared.tile([P, TILES, P, PACK], BF16, name="g_grouped", align_bytes=64, offset=2048)
+        g_codes = keep.tile([P, ROWS], U32, name="g_codes", align_bytes=64)
+        g_scales = keep.tile([P, ROWS], U8, name="g_scales", align_bytes=64)
+
+        scores = [product(q_codes, q_scales, k_words, k_scales, j, "a%d" % j) for j in range(TILES)]
+        weights = []
+        curved = []
+
+        def weigh(j):
+            p_tile = keep.tile([P, PACK, P], F32, name="p%d" % j)
+            nc.scalar.activation(p_tile[:], scores[j], ACT.Exp, bias=neg_lse[:, j: j + 1])
+            u_tile = keep.tile([P, PACK, P], F32, name="u%d" % j)
+            nc.scalar.activation(u_tile[:], p_tile[:], ACT.Identity, bias=512.0, scale=neg_mult[:, j: j + 1])
+            w_tile = keep.tile([P, PACK, P], F32, name="w%d" % j)
+            nc.vector.tensor_tensor(w_tile[:], p_tile[:], u_tile[:], ALU.mult)
+            weights.append(w_tile)
+
+        dst, src = deal_views(g_grouped, g_raw[0], 0)
+        nc.scalar.activation(dst, src, ACT.Copy)
+        fade_col = keep.tile([P, PACK], F32, name="fade_col", tag="stage2", align_bytes=64)
+        nc.sync.dma_start(out=fade_col[:], in_=fade.rearrange("(p t) o -> p (t o)", t=PACK))
+        dst, src = deal_views(g_grouped, g_raw[1], 1)
+        nc.vector.tensor_copy(dst, src)
+        quantise(g_grouped, g_codes, g_scales, 0, 2)
+        quantise(g_grouped, g_codes, g_scales, 2, 4)
+        v_words = gather(v_pool, shared.tile([P, SLOTS], U16, name="v_words", align_bytes=64, offset=1024))
+        for j in range(TILES):
+            weigh(j)
+
+        total = psum.tile([P, PACK, P], F32, name="total")
+        for j in range(TILES):
+            grad = product(g_codes, g_scales, v_words, v_scales, j, ["d0", "d1", "d2", "a0"][j])
+            s_tile = keep.tile([P, PACK, P], F32, name="s%d" % j)
+            nc.scalar.activation(s_tile[:], grad, ACT.Square)
+            c_tile = keep.tile([P, PACK, P], F32, name="c%d" % j)
+            nc.vector.tensor_tensor(c_tile[:], weights[j][:], s_tile[:], ALU.mult)
+            curved.append(c_tile)
+        for j in range(TILES):
+            for t in range(PACK):
+                nc.tensor.matmul(total[:, t, :], curved[j][:, t, :], identity[:], is_transpose=True,
+                                 start=(j == 0 and t == 0), stop=(j == TILES - 1 and t == PACK - 1))
+
+        pairs = total[:].rearrange("p t (g r) -> p t g r", r=2)
+        part = keep.tile([P, PACK, GROUPS], F32, name="part")
+        for t in range(PACK):
+            nc.vector.scalar_tensor_tensor(part[:, t, :], old_rows[:, t, :], fade_col[:, t: t + 1], pairs[:, t, :, 0],
+                                           ALU.mult, ALU.add)
+        y_grouped = keep.tile([P, GROUPS, PACK], BF16, name="y_grouped", align_bytes=64)
+        nc.vector.tensor_tensor(y_grouped[:], part[:].rearrange("p t g -> p g t"),
+                                pairs[:, :, :, 1].rearrange("p t g -> p g t"), ALU.add)
+        y_rows = keep.tile([P, PACK, GROUPS], F32, name="y_rows")
+        nc.vector.tensor_tensor(y_rows[:], part[:], pairs[:, :, :, 1], ALU.add)
+        y_codes = keep.tile([P, GROUPS], U32, name="y_codes", align_bytes=64)
+        y_scales = keep.tile([P, GROUPS], U8, name="y_scales", align_bytes=64)
+        nc.vector.quantize_mx(out=y_codes[:].bitcast(FP8X4), scales=y_scales[:],
+                              in_=y_grouped[:].rearrange("p g t -> p (g t)"))
+
+        nc.sync.dma_start(out=out_0.rearrange("(p t) g -> p t g", t=PACK), in_=y_rows[:])
+        nc.scalar.dma_start(out=out_1[0].rearrange("p c r -> p (c r)").bitcast(I32), in_=y_codes[:].bitcast(I32))
+        for quad in range(4):
+            queue = nc.sync if quad % 2 == 0 else nc.scalar
+            queue.dma_start(out=out_2[0, 4 * quad: 4 * quad + 4, :].bitcast(I32),
+                            in_=y_scales[32 * quad: 32 * quad + 4, :].bitcast(I32))

@@ -20,9 +20,9 @@ TOKENS = 2048
 SLOTS = 512
 ROWS = 512
 GROUPS = 64
+GROUP = 8
 TILES = ROWS // P
 HALF = ROWS // 2
-SHARE = 96
 FLOPS = 2 * 2 * 512 * SLOTS * ROWS
 
 
@@ -31,43 +31,49 @@ def tile_attend_curvatures_pl_kernel(tc, query, keys_words, keys_scales, lse, mu
     nc = tc.nc
     with ExitStack() as ctx:
         keep = ctx.enter_context(tc.tile_pool(name="keep", bufs=1))
-        shared = ctx.enter_context(tc.tile_pool(name="shared", bufs=1))
         psum = ctx.enter_context(tc.psum_pool(name="psum", bufs=1))
 
         offsets = keep.tile([P, SLOTS // 16], U16, name="offsets")
         nc.sync.dma_start(offsets[:], offs)
 
-        def load_words(words, name, tag):
-            pool_words = keep.tile([P, TOKENS], U16, name=name, tag=tag, align_bytes=64)
+        def load_words(words, name):
+            pool_words = keep.tile([P, TOKENS], U16, name=name, tag=name, align_bytes=64)
             nc.sync.dma_start(out=pool_words[:].bitcast(I32), in_=words[0].bitcast(I32))
             return pool_words
 
         def load_scales(scales, name, zero_engine, queue):
-            pool_scales = keep.tile([P, TOKENS], U8, name=name, tag=name, align_bytes=64)
+            pool_scales = keep.tile([P, TOKENS], U8, name=name, align_bytes=64)
             zero_engine.memset(pool_scales[:].bitcast(I32), 0)
             for quad in range(4):
                 queue.dma_start(out=pool_scales[32 * quad: 32 * quad + 4, :].bitcast(I32),
                                 in_=scales[0, 4 * quad: 4 * quad + 4, :].bitcast(I32))
             return pool_scales
 
-        def load_half(src, half, name, tag):
-            raw = keep.tile([P, PACK, HALF], F32, name=name, tag=tag, align_bytes=64)
+        def load_half(src, half, name):
+            raw = keep.tile([P, PACK, HALF], F32, name=name, tag=name)
             nc.sync.dma_start(out=raw[:], in_=src[:, half * HALF: (half + 1) * HALF].rearrange("(p t) q -> p t q", t=PACK))
             return raw
 
-        def gather(window, picked):
+        def load_row_values(vector, name, queue):
+            spread = keep.tile([P, GROUP - 1], F32, name=name)
+            by_group = vector.rearrange("o (g k) -> g (o k)", k=GROUP)
+            for r in range(2):
+                queue.dma_start(out=spread[r:P:2, :], in_=by_group[:, r: r + GROUP - 1])
+            return spread
+
+        def gather(window, dtype, name, tag):
+            picked = keep.tile([P, SLOTS], dtype, name=name, tag=tag, align_bytes=64)
             nc.vector.tensor_copy(picked[:], window[:].indirect(offsets[:]))
             return picked
 
-        def deal_views(grouped, raw, half, c0=0, c1=HALF):
-            m0, m1 = (half * HALF + c0) // TILES, (half * HALF + c1) // TILES
-            dst = grouped[:, :, m0:m1, :].rearrange("p j m t -> p m j t")
-            src = raw[:, :, c0:c1].rearrange("p t (m j) -> p m j t", j=TILES)
-            return dst, src
+        def deal(copy, grouped, raw, half, c0, c1):
+            g0, g1 = (half * HALF + c0) // GROUP, (half * HALF + c1) // GROUP
+            copy(grouped[:, :, g0:g1, :, :].rearrange("p j g r t -> p g j t r"),
+                 raw[:, :, c0:c1].rearrange("p t (g j r) -> p g j t r", j=TILES, r=2))
 
         def quantise(grouped, codes, scales, j0, j1):
             nc.vector.quantize_mx(out=codes[:, j0 * P: j1 * P].bitcast(FP8X4), scales=scales[:, j0 * P: j1 * P],
-                                  in_=grouped[:, j0:j1, :, :].rearrange("p j m t -> p (j m t)"))
+                                  in_=grouped[:, j0:j1, :, :, :].rearrange("p j g r t -> p (j g r t)"))
 
         def product(codes, scales, words, word_scales, j, tag):
             bank = psum.tile([P, SLOTS], F32, name="bank_%s" % tag, tag=tag)
@@ -76,78 +82,61 @@ def tile_attend_curvatures_pl_kernel(tc, query, keys_words, keys_scales, lse, mu
                                 rhs_scale=word_scales[:], start=True, stop=True)
             return bank[:].rearrange("p (s t) -> p t s", t=PACK)
 
-        warm = keep.tile([P, 2], F32, name="warm")
-        nc.gpsimd.memset(warm[:, 0:1], 0.0)
-        nc.scalar.activation(warm[:, 1:2], warm[:, 0:1], ACT.Exp)
-        lse_col = keep.tile([P, TILES], F32, name="lse_col", tag="stage1", align_bytes=64)
-        mult_col = keep.tile([P, TILES], F32, name="mult_col", tag="stage2", align_bytes=64)
-        nc.scalar.dma_start(out=lse_col[:], in_=lse.rearrange("o (p j) -> p (o j)", j=TILES))
-        nc.scalar.dma_start(out=mult_col[:], in_=mult.rearrange("o (p j) -> p (o j)", j=TILES))
-
-        k_pool = load_words(keys_words, "k_pool", "stage3")
-        ks_pool = load_scales(keys_scales, "ks_pool", nc.gpsimd, nc.scalar)
-        q_raw = [load_half(query, 0, "q_raw0", "stage0")]
-        vs_pool = load_scales(vals_scales, "vs_pool", nc.vector, nc.scalar)
-
+        fade_col = keep.tile([P, PACK], F32, name="fade_col")
+        nc.scalar.dma_start(out=fade_col[:], in_=fade.rearrange("(p t) o -> p (t o)", t=PACK))
+        vs_pool = keep.tile([P, TOKENS], U8, name="vs_pool", align_bytes=64)
+        nc.gpsimd.memset(vs_pool[:].bitcast(I32), 0)
+        nc.scalar.dma_start(out=vs_pool[0:P:8, :].bitcast(I32), in_=vals_scales[0].bitcast(I32))
+        ks_pool = load_scales(keys_scales, "ks_pool", nc.vector, nc.scalar)
+        lse_spread = load_row_values(lse, "lse_spread", nc.gpsimd)
         neg_lse = keep.tile([P, TILES], F32, name="neg_lse")
-        neg_mult = keep.tile([P, TILES], F32, name="neg_mult")
-        nc.vector.tensor_scalar(neg_lse[:], lse_col[:], -1.0, None, ALU.mult)
-        nc.vector.tensor_scalar(neg_mult[:], mult_col[:], -512.0, None, ALU.mult)
-        q_raw.append(load_half(query, 1, "q_raw1", "stage1"))
-        g_raw = [load_half(gout, 0, "g_raw0", "stage2")]
-
-        k_words = gather(k_pool, keep.tile([P, SLOTS], U16, name="k_words", align_bytes=64))
-        k_scales = gather(ks_pool, keep.tile([P, SLOTS], U8, name="k_scales", align_bytes=64))
-        g_raw.append(load_half(gout, 1, "g_raw1", "stage3"))
-
-        q_grouped = shared.tile([P, TILES, P, PACK], BF16, name="q_grouped", align_bytes=64, offset=0)
-        dst, src = deal_views(q_grouped, q_raw[0], 0)
-        nc.scalar.activation(dst, src, ACT.Copy)
-        v_pool = load_words(vals_words, "v_pool", "stage0")
-        dst, src = deal_views(q_grouped, q_raw[1], 1, 0, SHARE)
-        nc.scalar.activation(dst, src, ACT.Copy)
-        dst, src = deal_views(q_grouped, q_raw[1], 1, SHARE, HALF)
-        nc.vector.tensor_copy(dst, src)
-        old_rows = keep.tile([P, PACK, GROUPS], F32, name="old_rows", tag="stage1", align_bytes=64)
+        nc.scalar.activation(neg_lse[:], lse_spread[:, 0: GROUP - 1: 2], ACT.Identity, scale=-1.0)
+        mult_spread = load_row_values(mult, "mult_spread", nc.gpsimd)
+        q_raw = [load_half(query, 0, "q_raw0")]
+        k_pool = load_words(keys_words, "k_pool")
+        q_raw.append(load_half(query, 1, "q_raw1"))
+        g_raw = [load_half(gout, half, "g_raw%d" % half) for half in range(2)]
+        v_pool = load_words(vals_words, "v_pool")
+        old_rows = keep.tile([P, PACK, GROUPS], F32, name="old_rows")
         nc.sync.dma_start(out=old_rows[:], in_=old.rearrange("(p t) g -> p t g", t=PACK))
-
+        v_scales = keep.tile([P, SLOTS], U8, name="v_scales", align_bytes=64)
+        nc.gpsimd.memset(v_scales[:].bitcast(I32), 0)
         identity = keep.tile([P, P], F32, name="identity")
         make_identity(nc, identity[:])
+
+        vs_picked = gather(vs_pool, U8, "vs_picked", "vs_picked")
+        for r in range(4):
+            nc.sync.dma_start(out=v_scales[r:P:32, :].bitcast(I32), in_=vs_picked[8 * r: P: 32, :].bitcast(I32))
+        k_words = gather(k_pool, U16, "k_words", "k_words")
+        k_scales = gather(ks_pool, U8, "k_scales", "k_scales")
+
+        q_grouped = keep.tile([P, TILES, GROUPS, 2, PACK], BF16, name="q_grouped", tag="q_grouped", align_bytes=64)
+        deal(nc.scalar.copy, q_grouped, q_raw[0], 0, 0, HALF)
+        deal(nc.scalar.copy, q_grouped, q_raw[1], 1, 0, HALF)
 
         q_codes = keep.tile([P, ROWS], U32, name="q_codes", align_bytes=64)
         q_scales = keep.tile([P, ROWS], U8, name="q_scales", align_bytes=64)
         quantise(q_grouped, q_codes, q_scales, 0, 2)
         quantise(q_grouped, q_codes, q_scales, 2, 4)
-        v_scales = gather(vs_pool, shared.tile([P, SLOTS], U8, name="v_scales", align_bytes=64, offset=0))
+        scores = [product(q_codes, q_scales, k_words, k_scales, j, "a%d" % j) for j in range(TILES)]
 
-        g_grouped = shared.tile([P, TILES, P, PACK], BF16, name="g_grouped", align_bytes=64, offset=2048)
+        g_grouped = keep.tile([P, TILES, GROUPS, 2, PACK], BF16, name="g_grouped", align_bytes=64)
         g_codes = keep.tile([P, ROWS], U32, name="g_codes", align_bytes=64)
         g_scales = keep.tile([P, ROWS], U8, name="g_scales", align_bytes=64)
-
-        scores = [product(q_codes, q_scales, k_words, k_scales, j, "a%d" % j) for j in range(TILES)]
-        weights = []
-        curved = []
-
-        def weigh(j):
-            p_tile = keep.tile([P, PACK, P], F32, name="p%d" % j)
-            nc.scalar.activation(p_tile[:], scores[j], ACT.Exp, bias=neg_lse[:, j: j + 1])
-            u_tile = keep.tile([P, PACK, P], F32, name="u%d" % j)
-            nc.scalar.activation(u_tile[:], p_tile[:], ACT.Identity, bias=512.0, scale=neg_mult[:, j: j + 1])
-            w_tile = keep.tile([P, PACK, P], F32, name="w%d" % j)
-            nc.vector.tensor_tensor(w_tile[:], p_tile[:], u_tile[:], ALU.mult)
-            weights.append(w_tile)
-
-        dst, src = deal_views(g_grouped, g_raw[0], 0)
-        nc.scalar.activation(dst, src, ACT.Copy)
-        fade_col = keep.tile([P, PACK], F32, name="fade_col", tag="stage2", align_bytes=64)
-        nc.sync.dma_start(out=fade_col[:], in_=fade.rearrange("(p t) o -> p (t o)", t=PACK))
-        dst, src = deal_views(g_grouped, g_raw[1], 1)
-        nc.vector.tensor_copy(dst, src)
+        deal(nc.scalar.copy, g_grouped, g_raw[0], 0, 0, HALF)
+        deal(nc.vector.tensor_copy, g_grouped, g_raw[1], 1, 0, HALF)
         quantise(g_grouped, g_codes, g_scales, 0, 2)
         quantise(g_grouped, g_codes, g_scales, 2, 4)
-        v_words = gather(v_pool, shared.tile([P, SLOTS], U16, name="v_words", align_bytes=64, offset=1024))
+        v_words = gather(v_pool, U16, "v_words", "v_words")
+
+        weights = keep.tile([P, TILES, PACK, P], F32, name="weights", tag="v_pool", align_bytes=64)
+        probs = keep.tile([P, TILES, PACK, P], F32, name="probs", tag="g_raw0")
+        curved = []
         for j in range(TILES):
-            weigh(j)
+            nc.scalar.activation(probs[:, j, :, :], scores[j], ACT.Exp, bias=neg_lse[:, j: j + 1])
+            u_tile = keep.tile([P, PACK, P], F32, name="u%d" % j)
+            nc.scalar.activation(u_tile[:], probs[:, j, :, :], ACT.Identity, bias=-1.0, scale=mult_spread[:, 2 * j: 2 * j + 1])
+            nc.vector.scalar_tensor_tensor(weights[:, j, :, :], probs[:, j, :, :], -512.0, u_tile[:], ALU.mult, ALU.mult)
 
         total = psum.tile([P, PACK, P], F32, name="total")
         for j in range(TILES):
@@ -155,7 +144,10 @@ def tile_attend_curvatures_pl_kernel(tc, query, keys_words, keys_scales, lse, mu
             s_tile = keep.tile([P, PACK, P], F32, name="s%d" % j)
             nc.scalar.activation(s_tile[:], grad, ACT.Square)
             c_tile = keep.tile([P, PACK, P], F32, name="c%d" % j)
-            nc.vector.tensor_tensor(c_tile[:], weights[j][:], s_tile[:], ALU.mult)
+            step = 2 if j == TILES - 1 else PACK
+            for t0 in range(0, PACK, step):
+                nc.vector.tensor_tensor(c_tile[:, t0: t0 + step, :], weights[:, j, t0: t0 + step, :],
+                                        s_tile[:, t0: t0 + step, :], ALU.mult)
             curved.append(c_tile)
         for j in range(TILES):
             for t in range(PACK):

@@ -22,7 +22,7 @@ ROWS = 512
 GROUPS = 64
 GROUP = 8
 TILES = ROWS // P
-HALF = ROWS // 2
+SHARE = 128
 FLOPS = 2 * 2 * 512 * SLOTS * ROWS
 
 
@@ -38,37 +38,43 @@ def tile_attend_curvatures_pl_kernel(tc, query, keys_words, keys_scales, lse, mu
 
         def load_words(words, name):
             pool_words = keep.tile([P, TOKENS], U16, name=name, tag=name, align_bytes=64)
-            nc.sync.dma_start(out=pool_words[:].bitcast(I32), in_=words[0].bitcast(I32))
+            nc.scalar.dma_start(out=pool_words[:].bitcast(I32), in_=words[0].bitcast(I32))
             return pool_words
 
-        def load_scales(scales, name, zero_engine, queue):
-            pool_scales = keep.tile([P, TOKENS], U8, name=name, align_bytes=64)
+        def load_scales(scales, name, zero_engine):
+            pool_scales = keep.tile([P, TOKENS], U8, name=name, tag=name, align_bytes=64)
             zero_engine.memset(pool_scales[:].bitcast(I32), 0)
-            for quad in range(4):
-                queue.dma_start(out=pool_scales[32 * quad: 32 * quad + 4, :].bitcast(I32),
-                                in_=scales[0, 4 * quad: 4 * quad + 4, :].bitcast(I32))
+            nc.sync.dma_start(out=pool_scales[0:P:8, :].bitcast(I32), in_=scales[0].bitcast(I32))
             return pool_scales
 
-        def load_half(src, half, name):
-            raw = keep.tile([P, PACK, HALF], F32, name=name, tag=name)
-            nc.sync.dma_start(out=raw[:], in_=src[:, half * HALF: (half + 1) * HALF].rearrange("(p t) q -> p t q", t=PACK))
+        def load_rows(src, name):
+            raw = keep.tile([P, PACK, ROWS], F32, name=name, tag=name)
+            nc.scalar.dma_start(out=raw[:], in_=src.rearrange("(p t) q -> p t q", t=PACK))
             return raw
 
-        def load_row_values(vector, name, queue):
-            spread = keep.tile([P, GROUP - 1], F32, name=name)
+        def load_row_values(vector, name, tag):
+            spread = keep.tile([P, GROUP - 1], F32, name=name, tag=tag, align_bytes=64)
             by_group = vector.rearrange("o (g k) -> g (o k)", k=GROUP)
             for r in range(2):
-                queue.dma_start(out=spread[r:P:2, :], in_=by_group[:, r: r + GROUP - 1])
+                nc.sync.dma_start(out=spread[r:P:2, :], in_=by_group[:, r: r + GROUP - 1])
             return spread
+
+        def zeroed_plane(name):
+            plane = keep.tile([P, SLOTS], U8, name=name, align_bytes=64)
+            nc.gpsimd.memset(plane[:].bitcast(I32), 0)
+            return plane
+
+        def place_scales(picked, plane):
+            for r in range(4):
+                nc.sync.dma_start(out=plane[r:P:32, :].bitcast(I32), in_=picked[8 * r: P: 32, :].bitcast(I32))
 
         def gather(window, dtype, name, tag):
             picked = keep.tile([P, SLOTS], dtype, name=name, tag=tag, align_bytes=64)
             nc.vector.tensor_copy(picked[:], window[:].indirect(offsets[:]))
             return picked
 
-        def deal(copy, grouped, raw, half, c0, c1):
-            g0, g1 = (half * HALF + c0) // GROUP, (half * HALF + c1) // GROUP
-            copy(grouped[:, :, g0:g1, :, :].rearrange("p j g r t -> p g j t r"),
+        def deal(copy, grouped, raw, c0, c1):
+            copy(grouped[:, :, c0 // GROUP: c1 // GROUP, :, :].rearrange("p j g r t -> p g j t r"),
                  raw[:, :, c0:c1].rearrange("p t (g j r) -> p g j t r", j=TILES, r=2))
 
         def quantise(grouped, codes, scales, j0, j1):
@@ -82,55 +88,49 @@ def tile_attend_curvatures_pl_kernel(tc, query, keys_words, keys_scales, lse, mu
                                 rhs_scale=word_scales[:], start=True, stop=True)
             return bank[:].rearrange("p (s t) -> p t s", t=PACK)
 
-        fade_col = keep.tile([P, PACK], F32, name="fade_col")
-        nc.scalar.dma_start(out=fade_col[:], in_=fade.rearrange("(p t) o -> p (t o)", t=PACK))
-        vs_pool = keep.tile([P, TOKENS], U8, name="vs_pool", align_bytes=64)
-        nc.gpsimd.memset(vs_pool[:].bitcast(I32), 0)
-        nc.scalar.dma_start(out=vs_pool[0:P:8, :].bitcast(I32), in_=vals_scales[0].bitcast(I32))
-        ks_pool = load_scales(keys_scales, "ks_pool", nc.vector, nc.scalar)
-        lse_spread = load_row_values(lse, "lse_spread", nc.gpsimd)
+        q_raw = load_rows(query, "q_raw")
+        k_pool = load_words(keys_words, "k_pool")
+        g_raw = load_rows(gout, "g_raw")
+        lse_spread = load_row_values(lse, "lse_spread", "lse_spread")
+        ks_pool = load_scales(keys_scales, "ks_pool", nc.gpsimd)
+        vs_pool = load_scales(vals_scales, "vs_pool", nc.vector)
         neg_lse = keep.tile([P, TILES], F32, name="neg_lse")
         nc.scalar.activation(neg_lse[:], lse_spread[:, 0: GROUP - 1: 2], ACT.Identity, scale=-1.0)
-        mult_spread = load_row_values(mult, "mult_spread", nc.gpsimd)
-        q_raw = [load_half(query, 0, "q_raw0")]
-        k_pool = load_words(keys_words, "k_pool")
-        q_raw.append(load_half(query, 1, "q_raw1"))
-        g_raw = [load_half(gout, half, "g_raw%d" % half) for half in range(2)]
         v_pool = load_words(vals_words, "v_pool")
-        old_rows = keep.tile([P, PACK, GROUPS], F32, name="old_rows")
-        nc.sync.dma_start(out=old_rows[:], in_=old.rearrange("(p t) g -> p t g", t=PACK))
-        v_scales = keep.tile([P, SLOTS], U8, name="v_scales", align_bytes=64)
-        nc.gpsimd.memset(v_scales[:].bitcast(I32), 0)
+        k_scales = zeroed_plane("k_scales")
+        v_scales = zeroed_plane("v_scales")
         identity = keep.tile([P, P], F32, name="identity")
         make_identity(nc, identity[:])
 
+        place_scales(gather(ks_pool, U8, "ks_picked", "ks_picked"), k_scales)
         vs_picked = gather(vs_pool, U8, "vs_picked", "vs_picked")
-        for r in range(4):
-            nc.sync.dma_start(out=v_scales[r:P:32, :].bitcast(I32), in_=vs_picked[8 * r: P: 32, :].bitcast(I32))
+        mult_spread = load_row_values(mult, "mult_spread", "vs_pool")
+        place_scales(vs_picked, v_scales)
         k_words = gather(k_pool, U16, "k_words", "k_words")
-        k_scales = gather(ks_pool, U8, "k_scales", "k_scales")
+        old_rows = keep.tile([P, PACK, GROUPS], F32, name="old_rows", tag="k_pool", align_bytes=64)
+        nc.sync.dma_start(out=old_rows[:], in_=old.rearrange("(p t) g -> p t g", t=PACK))
+        fade_col = keep.tile([P, PACK], F32, name="fade_col", tag="lse_spread", align_bytes=64)
+        nc.sync.dma_start(out=fade_col[:], in_=fade.rearrange("(p t) o -> p (t o)", t=PACK))
 
-        q_grouped = keep.tile([P, TILES, GROUPS, 2, PACK], BF16, name="q_grouped", tag="q_grouped", align_bytes=64)
-        deal(nc.scalar.copy, q_grouped, q_raw[0], 0, 0, HALF)
-        deal(nc.scalar.copy, q_grouped, q_raw[1], 1, 0, HALF)
+        q_grouped = keep.tile([P, TILES, GROUPS, 2, PACK], BF16, name="q_grouped", tag="grouped", align_bytes=64)
+        deal(nc.scalar.copy, q_grouped, q_raw, 0, ROWS)
 
         q_codes = keep.tile([P, ROWS], U32, name="q_codes", align_bytes=64)
         q_scales = keep.tile([P, ROWS], U8, name="q_scales", align_bytes=64)
-        quantise(q_grouped, q_codes, q_scales, 0, 2)
-        quantise(q_grouped, q_codes, q_scales, 2, 4)
+        quantise(q_grouped, q_codes, q_scales, 0, 4)
         scores = [product(q_codes, q_scales, k_words, k_scales, j, "a%d" % j) for j in range(TILES)]
 
-        g_grouped = keep.tile([P, TILES, GROUPS, 2, PACK], BF16, name="g_grouped", align_bytes=64)
+        g_grouped = keep.tile([P, TILES, GROUPS, 2, PACK], BF16, name="g_grouped", tag="grouped", align_bytes=64)
         g_codes = keep.tile([P, ROWS], U32, name="g_codes", align_bytes=64)
         g_scales = keep.tile([P, ROWS], U8, name="g_scales", align_bytes=64)
-        deal(nc.scalar.copy, g_grouped, g_raw[0], 0, 0, HALF)
-        deal(nc.vector.tensor_copy, g_grouped, g_raw[1], 1, 0, HALF)
+        deal(nc.scalar.copy, g_grouped, g_raw, 0, SHARE)
+        deal(nc.vector.tensor_copy, g_grouped, g_raw, SHARE, ROWS)
         quantise(g_grouped, g_codes, g_scales, 0, 2)
         quantise(g_grouped, g_codes, g_scales, 2, 4)
-        v_words = gather(v_pool, U16, "v_words", "v_words")
+        v_words = gather(v_pool, U16, "v_words", "grouped")
 
         weights = keep.tile([P, TILES, PACK, P], F32, name="weights", tag="v_pool", align_bytes=64)
-        probs = keep.tile([P, TILES, PACK, P], F32, name="probs", tag="g_raw0")
+        probs = keep.tile([P, TILES, PACK, P], F32, name="probs")
         curved = []
         for j in range(TILES):
             nc.scalar.activation(probs[:, j, :, :], scores[j], ACT.Exp, bias=neg_lse[:, j: j + 1])
@@ -142,10 +142,10 @@ def tile_attend_curvatures_pl_kernel(tc, query, keys_words, keys_scales, lse, mu
         for j in range(TILES):
             grad = product(g_codes, g_scales, v_words, v_scales, j, ["d0", "d1", "d2", "a0"][j])
             s_tile = keep.tile([P, PACK, P], F32, name="s%d" % j)
-            nc.scalar.activation(s_tile[:], grad, ACT.Square)
             c_tile = keep.tile([P, PACK, P], F32, name="c%d" % j)
             step = 2 if j == TILES - 1 else PACK
             for t0 in range(0, PACK, step):
+                nc.scalar.activation(s_tile[:, t0: t0 + step, :], grad[:, t0: t0 + step, :], ACT.Square)
                 nc.vector.tensor_tensor(c_tile[:, t0: t0 + step, :], weights[:, j, t0: t0 + step, :],
                                         s_tile[:, t0: t0 + step, :], ALU.mult)
             curved.append(c_tile)

@@ -22,7 +22,8 @@ ROWS = 512
 GROUPS = 64
 GROUP = 8
 TILES = ROWS // P
-SHARE = 128
+QUERY_SHARE = 256
+SHARE = 96
 FLOPS = 2 * 2 * 512 * SLOTS * ROWS
 
 
@@ -38,35 +39,20 @@ def tile_attend_curvatures_pl_kernel(tc, query, keys_words, keys_scales, lse, mu
 
         def load_words(words, name):
             pool_words = keep.tile([P, TOKENS], U16, name=name, tag=name, align_bytes=64)
-            nc.scalar.dma_start(out=pool_words[:].bitcast(I32), in_=words[0].bitcast(I32))
+            nc.sync.dma_start(out=pool_words[:].bitcast(I32), in_=words[0].bitcast(I32))
             return pool_words
-
-        def load_scales(scales, name, zero_engine):
-            pool_scales = keep.tile([P, TOKENS], U8, name=name, tag=name, align_bytes=64)
-            zero_engine.memset(pool_scales[:].bitcast(I32), 0)
-            nc.sync.dma_start(out=pool_scales[0:P:8, :].bitcast(I32), in_=scales[0].bitcast(I32))
-            return pool_scales
 
         def load_rows(src, name):
             raw = keep.tile([P, PACK, ROWS], F32, name=name, tag=name)
-            nc.scalar.dma_start(out=raw[:], in_=src.rearrange("(p t) q -> p t q", t=PACK))
+            nc.sync.dma_start(out=raw[:], in_=src.rearrange("(p t) q -> p t q", t=PACK))
             return raw
 
-        def load_row_values(vector, name, tag):
-            spread = keep.tile([P, GROUP - 1], F32, name=name, tag=tag, align_bytes=64)
+        def load_row_values(vector, name):
+            spread = keep.tile([P, GROUP - 1], F32, name=name)
             by_group = vector.rearrange("o (g k) -> g (o k)", k=GROUP)
             for r in range(2):
                 nc.sync.dma_start(out=spread[r:P:2, :], in_=by_group[:, r: r + GROUP - 1])
             return spread
-
-        def zeroed_plane(name):
-            plane = keep.tile([P, SLOTS], U8, name=name, align_bytes=64)
-            nc.gpsimd.memset(plane[:].bitcast(I32), 0)
-            return plane
-
-        def place_scales(picked, plane):
-            for r in range(4):
-                nc.sync.dma_start(out=plane[r:P:32, :].bitcast(I32), in_=picked[8 * r: P: 32, :].bitcast(I32))
 
         def gather(window, dtype, name, tag):
             picked = keep.tile([P, SLOTS], dtype, name=name, tag=tag, align_bytes=64)
@@ -88,32 +74,43 @@ def tile_attend_curvatures_pl_kernel(tc, query, keys_words, keys_scales, lse, mu
                                 rhs_scale=word_scales[:], start=True, stop=True)
             return bank[:].rearrange("p (s t) -> p t s", t=PACK)
 
-        q_raw = load_rows(query, "q_raw")
         k_pool = load_words(keys_words, "k_pool")
+        vs_pool = keep.tile([P, TOKENS], U8, name="vs_pool", align_bytes=64)
+        nc.gpsimd.memset(vs_pool[:].bitcast(I32), 0)
+        nc.sync.dma_start(out=vs_pool[0:P:8, :].bitcast(I32), in_=vals_scales[0].bitcast(I32))
+        ks_pool = keep.tile([P, TOKENS], U8, name="ks_pool", align_bytes=64)
+        nc.vector.memset(ks_pool[:].bitcast(I32), 0)
+        for quad in range(4):
+            nc.sync.dma_start(out=ks_pool[32 * quad: 32 * quad + 4, :].bitcast(I32),
+                              in_=keys_scales[0, 4 * quad: 4 * quad + 4, :].bitcast(I32))
+        q_raw = load_rows(query, "q_raw")
+        lse_spread = load_row_values(lse, "lse_spread")
         g_raw = load_rows(gout, "g_raw")
-        lse_spread = load_row_values(lse, "lse_spread", "lse_spread")
-        ks_pool = load_scales(keys_scales, "ks_pool", nc.gpsimd)
-        vs_pool = load_scales(vals_scales, "vs_pool", nc.vector)
-        neg_lse = keep.tile([P, TILES], F32, name="neg_lse")
-        nc.scalar.activation(neg_lse[:], lse_spread[:, 0: GROUP - 1: 2], ACT.Identity, scale=-1.0)
+        mult_spread = load_row_values(mult, "mult_spread")
         v_pool = load_words(vals_words, "v_pool")
-        k_scales = zeroed_plane("k_scales")
-        v_scales = zeroed_plane("v_scales")
-        identity = keep.tile([P, P], F32, name="identity")
-        make_identity(nc, identity[:])
-
-        place_scales(gather(ks_pool, U8, "ks_picked", "ks_picked"), k_scales)
-        vs_picked = gather(vs_pool, U8, "vs_picked", "vs_picked")
-        mult_spread = load_row_values(mult, "mult_spread", "vs_pool")
-        place_scales(vs_picked, v_scales)
-        k_words = gather(k_pool, U16, "k_words", "k_words")
-        old_rows = keep.tile([P, PACK, GROUPS], F32, name="old_rows", tag="k_pool", align_bytes=64)
+        old_rows = keep.tile([P, PACK, GROUPS], F32, name="old_rows")
         nc.sync.dma_start(out=old_rows[:], in_=old.rearrange("(p t) g -> p t g", t=PACK))
-        fade_col = keep.tile([P, PACK], F32, name="fade_col", tag="lse_spread", align_bytes=64)
+        fade_col = keep.tile([P, PACK], F32, name="fade_col")
         nc.sync.dma_start(out=fade_col[:], in_=fade.rearrange("(p t) o -> p (t o)", t=PACK))
 
-        q_grouped = keep.tile([P, TILES, GROUPS, 2, PACK], BF16, name="q_grouped", tag="grouped", align_bytes=64)
-        deal(nc.scalar.copy, q_grouped, q_raw, 0, ROWS)
+        identity_bf16 = keep.tile([P, P], BF16, name="identity_bf16")
+        make_identity(nc, identity_bf16[:])
+        identity = keep.tile([P, P], F32, name="identity")
+        nc.scalar.activation(identity[:], identity_bf16[:], ACT.Identity)
+        v_scales = keep.tile([P, SLOTS], U8, name="v_scales", align_bytes=64)
+        nc.gpsimd.memset(v_scales[:].bitcast(I32), 0)
+
+        k_words = gather(k_pool, U16, "k_words", "k_words")
+        vs_picked = gather(vs_pool, U8, "vs_picked", "vs_picked")
+        for r in range(4):
+            nc.sync.dma_start(out=v_scales[r:P:32, :].bitcast(I32), in_=vs_picked[8 * r: P: 32, :].bitcast(I32))
+        k_scales = gather(ks_pool, U8, "k_scales", "k_scales")
+        neg_lse = keep.tile([P, TILES], F32, name="neg_lse")
+        nc.vector.tensor_scalar(neg_lse[:], lse_spread[:, 0: GROUP - 1: 2], -1.0, None, ALU.mult)
+
+        q_grouped = keep.tile([P, TILES, GROUPS, 2, PACK], BF16, name="q_grouped", align_bytes=64)
+        deal(nc.scalar.copy, q_grouped, q_raw, 0, QUERY_SHARE)
+        deal(nc.vector.tensor_copy, q_grouped, q_raw, QUERY_SHARE, ROWS)
 
         q_codes = keep.tile([P, ROWS], U32, name="q_codes", align_bytes=64)
         q_scales = keep.tile([P, ROWS], U8, name="q_scales", align_bytes=64)

from contextlib import ExitStack

import concourse.mybir as mybir
from concourse.masks import make_identity

F32 = mybir.dt.float32
BF16 = mybir.dt.bfloat16
I32 = mybir.dt.int32
U32 = mybir.dt.uint32
U16 = mybir.dt.uint16
U8 = mybir.dt.uint8
FP8X4 = mybir.dt.float8_e4m3fn_x4
FP4X4 = mybir.dt.float4_e2m1fn_x4
ACT = mybir.ActivationFunctionType
ALU = mybir.AluOpType

P = 128
PACK = 4
TOKENS = 2048
SLOTS = 512
ROWS = 512
GROUPS = 64
GROUP = 8
TILES = ROWS // P
QUERY_SHARE = 256
SHARE = 96
FLOPS = 2 * 2 * 512 * SLOTS * ROWS


def tile_attend_curvatures_pl_kernel(tc, query, keys_words, keys_scales, lse, mult, gout, vals_words, vals_scales,
                                      old, fade, offs, out_0, out_1, out_2):
    nc = tc.nc
    with ExitStack() as ctx:
        keep = ctx.enter_context(tc.tile_pool(name="keep", bufs=1))
        psum = ctx.enter_context(tc.psum_pool(name="psum", bufs=1))

        offsets = keep.tile([P, SLOTS // 16], U16, name="offsets")
        nc.sync.dma_start(offsets[:], offs)

        def load_words(words, name):
            pool_words = keep.tile([P, TOKENS], U16, name=name, tag=name, align_bytes=64)
            nc.sync.dma_start(out=pool_words[:].bitcast(I32), in_=words[0].bitcast(I32))
            return pool_words

        def load_rows(src, name):
            raw = keep.tile([P, PACK, ROWS], F32, name=name, tag=name)
            nc.sync.dma_start(out=raw[:], in_=src.rearrange("(p t) q -> p t q", t=PACK))
            return raw

        def load_row_values(vector, name):
            spread = keep.tile([P, GROUP - 1], F32, name=name)
            by_group = vector.rearrange("o (g k) -> g (o k)", k=GROUP)
            for r in range(2):
                nc.sync.dma_start(out=spread[r:P:2, :], in_=by_group[:, r: r + GROUP - 1])
            return spread

        def gather(window, dtype, name, tag):
            picked = keep.tile([P, SLOTS], dtype, name=name, tag=tag, align_bytes=64)
            nc.vector.tensor_copy(picked[:], window[:].indirect(offsets[:]))
            return picked

        def deal(copy, grouped, raw, c0, c1):
            copy(grouped[:, :, c0 // GROUP: c1 // GROUP, :, :].rearrange("p j g r t -> p g j t r"),
                 raw[:, :, c0:c1].rearrange("p t (g j r) -> p g j t r", j=TILES, r=2))

        def quantise(grouped, codes, scales, j0, j1):
            nc.vector.quantize_mx(out=codes[:, j0 * P: j1 * P].bitcast(FP8X4), scales=scales[:, j0 * P: j1 * P],
                                  in_=grouped[:, j0:j1, :, :, :].rearrange("p j g r t -> p (j g r t)"))

        def product(codes, scales, words, word_scales, j, tag):
            bank = psum.tile([P, SLOTS], F32, name="bank_%s" % tag, tag=tag)
            nc.tensor.matmul_mx(out=bank[:], lhsT=codes[:, j * P: (j + 1) * P].bitcast(FP8X4),
                                lhsT_scale=scales[:, j * P: (j + 1) * P], rhs=words[:].bitcast(FP4X4),
                                rhs_scale=word_scales[:], start=True, stop=True)
            return bank[:].rearrange("p (s t) -> p t s", t=PACK)

        k_pool = load_words(keys_words, "k_pool")
        vs_pool = keep.tile([P, TOKENS], U8, name="vs_pool", align_bytes=64)
        nc.gpsimd.memset(vs_pool[:].bitcast(I32), 0)
        nc.sync.dma_start(out=vs_pool[0:P:8, :].bitcast(I32), in_=vals_scales[0].bitcast(I32))
        ks_pool = keep.tile([P, TOKENS], U8, name="ks_pool", align_bytes=64)
        nc.vector.memset(ks_pool[:].bitcast(I32), 0)
        for quad in range(4):
            nc.sync.dma_start(out=ks_pool[32 * quad: 32 * quad + 4, :].bitcast(I32),
                              in_=keys_scales[0, 4 * quad: 4 * quad + 4, :].bitcast(I32))
        q_raw = load_rows(query, "q_raw")
        lse_spread = load_row_values(lse, "lse_spread")
        g_raw = load_rows(gout, "g_raw")
        mult_spread = load_row_values(mult, "mult_spread")
        v_pool = load_words(vals_words, "v_pool")
        old_rows = keep.tile([P, PACK, GROUPS], F32, name="old_rows")
        nc.sync.dma_start(out=old_rows[:], in_=old.rearrange("(p t) g -> p t g", t=PACK))
        fade_col = keep.tile([P, PACK], F32, name="fade_col")
        nc.sync.dma_start(out=fade_col[:], in_=fade.rearrange("(p t) o -> p (t o)", t=PACK))

        identity_bf16 = keep.tile([P, P], BF16, name="identity_bf16")
        make_identity(nc, identity_bf16[:])
        identity = keep.tile([P, P], F32, name="identity")
        nc.scalar.activation(identity[:], identity_bf16[:], ACT.Identity)
        v_scales = keep.tile([P, SLOTS], U8, name="v_scales", align_bytes=64)
        nc.gpsimd.memset(v_scales[:].bitcast(I32), 0)

        k_words = gather(k_pool, U16, "k_words", "k_words")
        vs_picked = gather(vs_pool, U8, "vs_picked", "vs_picked")
        for r in range(4):
            nc.sync.dma_start(out=v_scales[r:P:32, :].bitcast(I32), in_=vs_picked[8 * r: P: 32, :].bitcast(I32))
        k_scales = gather(ks_pool, U8, "k_scales", "k_scales")
        neg_lse = keep.tile([P, TILES], F32, name="neg_lse")
        nc.vector.tensor_scalar(neg_lse[:], lse_spread[:, 0: GROUP - 1: 2], -1.0, None, ALU.mult)

        q_grouped = keep.tile([P, TILES, GROUPS, 2, PACK], BF16, name="q_grouped", align_bytes=64)
        deal(nc.scalar.copy, q_grouped, q_raw, 0, QUERY_SHARE)
        deal(nc.vector.tensor_copy, q_grouped, q_raw, QUERY_SHARE, ROWS)

        q_codes = keep.tile([P, ROWS], U32, name="q_codes", align_bytes=64)
        q_scales = keep.tile([P, ROWS], U8, name="q_scales", align_bytes=64)
        quantise(q_grouped, q_codes, q_scales, 0, 4)
        scores = [product(q_codes, q_scales, k_words, k_scales, j, "a%d" % j) for j in range(TILES)]

        g_grouped = keep.tile([P, TILES, GROUPS, 2, PACK], BF16, name="g_grouped", tag="grouped", align_bytes=64)
        g_codes = keep.tile([P, ROWS], U32, name="g_codes", align_bytes=64)
        g_scales = keep.tile([P, ROWS], U8, name="g_scales", align_bytes=64)
        deal(nc.scalar.copy, g_grouped, g_raw, 0, SHARE)
        deal(nc.vector.tensor_copy, g_grouped, g_raw, SHARE, ROWS)
        quantise(g_grouped, g_codes, g_scales, 0, 2)
        quantise(g_grouped, g_codes, g_scales, 2, 4)
        v_words = gather(v_pool, U16, "v_words", "grouped")

        weights = keep.tile([P, TILES, PACK, P], F32, name="weights", tag="v_pool", align_bytes=64)
        probs = keep.tile([P, TILES, PACK, P], F32, name="probs")
        curved = []
        for j in range(TILES):
            nc.scalar.activation(probs[:, j, :, :], scores[j], ACT.Exp, bias=neg_lse[:, j: j + 1])
            u_tile = keep.tile([P, PACK, P], F32, name="u%d" % j)
            nc.scalar.activation(u_tile[:], probs[:, j, :, :], ACT.Identity, bias=-1.0, scale=mult_spread[:, 2 * j: 2 * j + 1])
            nc.vector.scalar_tensor_tensor(weights[:, j, :, :], probs[:, j, :, :], -512.0, u_tile[:], ALU.mult, ALU.mult)

        total = psum.tile([P, PACK, P], F32, name="total")
        for j in range(TILES):
            grad = product(g_codes, g_scales, v_words, v_scales, j, ["d0", "d1", "d2", "a0"][j])
            s_tile = keep.tile([P, PACK, P], F32, name="s%d" % j)
            c_tile = keep.tile([P, PACK, P], F32, name="c%d" % j)
            step = 2 if j == TILES - 1 else PACK
            for t0 in range(0, PACK, step):
                nc.scalar.activation(s_tile[:, t0: t0 + step, :], grad[:, t0: t0 + step, :], ACT.Square)
                nc.vector.tensor_tensor(c_tile[:, t0: t0 + step, :], weights[:, j, t0: t0 + step, :],
                                        s_tile[:, t0: t0 + step, :], ALU.mult)
            curved.append(c_tile)
        for j in range(TILES):
            for t in range(PACK):
                nc.tensor.matmul(total[:, t, :], curved[j][:, t, :], identity[:], is_transpose=True,
                                 start=(j == 0 and t == 0), stop=(j == TILES - 1 and t == PACK - 1))

        pairs = total[:].rearrange("p t (g r) -> p t g r", r=2)
        part = keep.tile([P, PACK, GROUPS], F32, name="part")
        for t in range(PACK):
            nc.vector.scalar_tensor_tensor(part[:, t, :], old_rows[:, t, :], fade_col[:, t: t + 1], pairs[:, t, :, 0],
                                           ALU.mult, ALU.add)
        y_grouped = keep.tile([P, GROUPS, PACK], BF16, name="y_grouped", align_bytes=64)
        nc.vector.tensor_tensor(y_grouped[:], part[:].rearrange("p t g -> p g t"),
                                pairs[:, :, :, 1].rearrange("p t g -> p g t"), ALU.add)
        y_rows = keep.tile([P, PACK, GROUPS], F32, name="y_rows")
        nc.vector.tensor_tensor(y_rows[:], part[:], pairs[:, :, :, 1], ALU.add)
        y_codes = keep.tile([P, GROUPS], U32, name="y_codes", align_bytes=64)
        y_scales = keep.tile([P, GROUPS], U8, name="y_scales", align_bytes=64)
        nc.vector.quantize_mx(out=y_codes[:].bitcast(FP8X4), scales=y_scales[:],
                              in_=y_grouped[:].rearrange("p g t -> p (g t)"))

        nc.sync.dma_start(out=out_0.rearrange("(p t) g -> p t g", t=PACK), in_=y_rows[:])
        nc.scalar.dma_start(out=out_1[0].rearrange("p c r -> p (c r)").bitcast(I32), in_=y_codes[:].bitcast(I32))
        for quad in range(4):
            queue = nc.sync if quad % 2 == 0 else nc.scalar
            queue.dma_start(out=out_2[0, 4 * quad: 4 * quad + 4, :].bitcast(I32),
                            in_=y_scales[32 * quad: 32 * quad + 4, :].bitcast(I32))
